import numpy as np, ml_dtypes
CORES = [50,52,122,124]
N = 4
import mx_ref
NC = 256
M = NC // N
BF = ml_dtypes.bfloat16
def cut(t, i, w=512):
    return t[:, w * i:w * i + w]
def term(a, B):
    return np.stack([mx_ref.matmul(mx_ref.quantize(cut(a, i)), B) for i in range(4)], axis=2).reshape(128, -1)
def setup_inputs(rng):
    def f(*shape):
        return mx_ref.flush((rng.standard_normal(shape, dtype=np.float32) * np.exp2(rng.integers(-2, 3, shape[:-1] + (1,)))).astype(BF))
    return {"a": f(N, 128, 4 * 512), "b": f(N, 128, 4 * NC)}
def setup_inputs_blocks(rng):
    d = setup_inputs(rng)
    for k in ("a", "b"): d[k] = mx_ref.spread(d[k], rng, 2)
    return d
def setup_inputs_wide(rng):
    d = setup_inputs(rng)
    for k in ("a", "b"): d[k] = mx_ref.flush((d[k].astype(np.float32) * np.exp2(rng.integers(-4, 5, (N, 1, 1))).astype(np.float32)).astype(BF))
    return d
def setup_inputs_lossless(rng):
    a = np.zeros((N, 128, 4 * 128, 4), np.float32)
    for r in range(N):
        k = rng.integers(0, 512, size=4 * 128)
        a[r, k // 4, np.arange(4 * 128), k % 4] = 1.0
    size = np.repeat(2.0 ** rng.integers(-4, 5, size=(1, 1, (4 * NC) // 4)), 4, axis=2)
    b = rng.integers(-1, 2, size=(N, 128, 4 * NC)) * size
    return {"a": a.reshape(N, 128, 4 * 512).astype(BF), "b": b.astype(np.float32).astype(BF)}
def reference(a, b):
    T = [term(a[r], mx_ref.quantize(b[r])) for r in range(N)]
    y = np.zeros((N, 128, 4 * M), np.float32)
    for c in range(N):
        y[c] = mx_ref.total([cut(T[r], c, 4 * M) for r in range(N)])
    return {"y": y}

@@ -1,0 +1,258 @@
+from concourse.bass import DstId, RemoteDMATransfer
+from concourse.mybir import dt, AluOpType, ActivationFunctionType
+
+N = 4
+PW = 64
+HW = 2 * PW
+B0 = 3 * PW
+B1 = B0 + N * PW
+
+SCRATCH = {
+    "a_sb": ("sbuf", [128, 2048], "bfloat16"),
+    "b_sb": ("sbuf", [128, 1024], "bfloat16"),
+    "aq": ("sbuf", [128, 512], "float8_e4m3fn_x4"),
+    "asc": ("sbuf", [128, 512], "uint8"),
+    "bq": ("sbuf", [128, B1 + 3 * PW], "float8_e4m3fn_x4"),
+    "bsc": ("sbuf", [128, B1 + 3 * PW], "uint8"),
+    "ones": ("sbuf", [128, 128], "bfloat16"),
+    "eye": ("sbuf", [128, 128], "bfloat16"),
+    "sel": ("sbuf", [128, 2048], "bfloat16"),
+    "wq": ("sbuf", [128, 512], "float8_e4m3fn_x4"),
+    "wsc": ("sbuf", [128, 512], "uint8"),
+    "e": ("sbuf", [128, 1024], "bfloat16"),
+    "tq": ("sbuf", [128, 256], "float8_e4m3fn_x4"),
+    "tsc": ("sbuf", [128, 256], "uint8"),
+    "ysb": ("sbuf", [128, 256], "float32"),
+    "ps": ("psum", [128, 4096], "float32"),
+}
+SEMAPHORES = (
+    ["ld_bf", "ld_bn"] + ["ld_a%d" % i for i in range(4)]
+    + ["s_ones", "s_zero", "s_eye", "s_selc", "s_w", "s_qbf", "s_qbn"] + ["s_qa%d" % i for i in range(4)]
+    + ["s_pf%d" % i for i in range(4)] + ["s_pn%d" % i for i in range(4)] + ["s_f%d" % i for i in range(4)]
+    + ["s_cfv", "s_cfs", "s_tf", "s_cnv", "s_cns", "s_tn", "s_yv", "s_ys", "s_st"]
+    + ["arr0", "arr1", "arr2", "rly_c", "rly_s", "sent"]
+)
+
+
+def _plan(T, topo):
+    cores = list(T.cores)
+    taken = set(cores)
+    relay = {}
+    for s in range(N):
+        for d in range(N):
+            if s == d or topo.may_write(cores[s], cores[d]):
+                continue
+            cand = [h for h in range(topo.CHIPS * topo.CORES_PER_CHIP)
+                    if h not in taken and topo.chip(h) == topo.chip(cores[s]) and topo.may_write(h, cores[d])]
+            cand.sort(key=lambda h: (topo.die(h) != topo.die(cores[s]), h))
+            relay[(s, d)] = cand[0]
+            taken.add(cand[0])
+    order = {}
+    for d in range(N):
+        snd = [s for s in range(N) if s != d]
+        snd.sort(key=lambda s: (topo.chip(cores[s]) != topo.chip(cores[d]), (s, d) in relay, s))
+        order[d] = snd
+    return relay, order
+
+
+def _near(T, topo, r):
+    return [x for x in range(N) if topo.chip(T.cores[x]) == topo.chip(T.cores[r])]
+
+
+def _land(T, topo, d, k):
+    half = d - _near(T, topo, d)[0]
+    return (B0 - PW - PW * k) if half == 0 else (B1 + PW * k)
+
+
+def _engines(topo, src, dst):
+    m = topo.mask(src, dst)
+    return [x for x in range(m.bit_length()) if (m >> x) & 1]
+
+
+def _send(g, T, topo, core, items, src_q, src_s):
+    per = min(len(_engines(topo, core, it[0])) for it in items) // len(items)
+    for what in range(2):
+        trs = []
+        for j, (dc, sem_c, sem_s, a, b) in enumerate(items):
+            mask = sum(1 << x for x in _engines(topo, core, dc)[j * per:(j + 1) * per])
+            rid, pid, _se = topo.addr(dc)
+            if what == 0:
+                src, dst, sem = src_q[:, a:a + PW].bitcast(dt.uint8), T.bq[:, b:b + PW].bitcast(dt.uint8), sem_c
+            else:
+                src, dst, sem = src_s[:, a:a + PW], T.bsc[:, b:b + PW], sem_s
+            trs.append((rid, pid, mask, sem, src, dst))
+        if len(trs) == 1:
+            rid, pid, mask, sem, src, dst = trs[0]
+            g.remote_dma(dst, src, sem, T.sem.sent, pid, rid, mask)
+        else:
+            g.remote_dma_fused(
+                [RemoteDMATransfer(dst_ids=[DstId(rid=rid, pnc=pid)], dma_engine_mask=mask, remote_sem=sem,
+                                   src=src, dst=dst) for (rid, pid, mask, sem, src, dst) in trs],
+                local_sem=T.sem.sent)
+    return per, 2 * per * len(items)
+
+
+def _per(topo, src, dsts):
+    return min(len(_engines(topo, src, d)) for d in dsts) // len(dsts)
+
+
+def rank_program(g, core, T, topo):
+    relay, order = _plan(T, topo)
+    cores = list(T.cores)
+    S = T.sem
+    rank = T.rank_of(core)
+
+    if rank is None:
+        for (s, d), h in relay.items():
+            if h != core:
+                continue
+            inc = _per(topo, cores[s], [relay[(s, x)] for x in range(N) if (s, x) in relay])
+            col = _land(T, topo, d, order[d].index(s))
+            arr = S["arr%d" % order[d].index(s)]
+            es = _engines(topo, core, cores[d])
+            mask = sum(1 << x for x in es)
+            rid, pid, _se = topo.addr(cores[d])
+            g.wait_ge(S.rly_c, inc)
+            g.remote_dma(T.bq[:, col:col + PW].bitcast(dt.uint8), T.bq[:, col:col + PW].bitcast(dt.uint8),
+                         arr, S.sent, pid, rid, mask)
+            g.wait_ge(S.rly_s, inc)
+            g.remote_dma(T.bsc[:, col:col + PW], T.bsc[:, col:col + PW], arr, S.sent, pid, rid, mask)
+            g.wait_ge(S.sent, 2 * len(es))
+        return
+
+    v, sc, te, sy = g.vector, g.scalar, g.tensor, g.sync
+    near = _near(T, topo, rank)
+    far = [x for x in range(N) if x not in near]
+    n0, f0 = near[0], far[0]
+    half = rank - n0
+    copy = ActivationFunctionType.Copy
+
+    def bank(k):
+        return T.ps[:, 512 * k:512 * k + HW]
+
+    def a_tile(i):
+        return T.aq[:, 128 * i:128 * i + 128], T.asc[:, 128 * i:128 * i + 128]
+
+    def b_half(first):
+        return T.bq[:, B0 + PW * first:B0 + PW * first + HW], T.bsc[:, B0 + PW * first:B0 + PW * first + HW]
+
+    def load_b(q, first, sem):
+        q.dma_start(T.b_sb[:, 4 * PW * first:4 * PW * first + 4 * HW],
+                    T.b[:, 4 * PW * first:4 * PW * first + 4 * HW]).then_inc(sem, 16)
+
+    def load_a(q, i):
+        q.dma_start(T.a_sb[:, 512 * i:512 * i + 512], T.a[:, 512 * i:512 * i + 512]).then_inc(S["ld_a%d" % i], 16)
+
+    load_b(sy, f0, S.ld_bf)
+    load_a(sc, 0)
+    load_a(sy, 1)
+    load_a(sc, 2)
+    load_a(sy, 3)
+    load_b(sc, n0, S.ld_bn)
+
+    v.memset(T.ones[:], 1.0).then_inc(S.s_ones, 1)
+    v.memset(T.sel[:], 0.0).then_inc(S.s_zero, 1)
+    g.wait_ge(S.s_ones, 1)
+    g.affine_select(T.eye[:], T.ones[:], [[-1, 128]], AluOpType.is_equal, 0.0, 0, 1).then_inc(S.s_eye, 1)
+    v.wait_ge(S.s_eye, 1)
+    v.wait_ge(S.s_zero, 1)
+    for t in range(4):
+        v.tensor_copy(T.sel[:, 512 * t + t:512 * (t + 1):4], T.eye[:]).then_inc(S.s_selc, 1)
+    v.wait_ge(S.s_selc, 4)
+    v.quantize_mx(T.wq[:], T.wsc[:], T.sel[:]).then_inc(S.s_w, 1)
+
+    def quant_b(first, ld, sem):
+        q, s = b_half(first)
+        v.wait_ge(ld, 16)
+        v.quantize_mx(q, s, T.b_sb[:, 4 * PW * first:4 * PW * first + 4 * HW]).then_inc(sem, 1)
+
+    quant_b(f0, S.ld_bf, S.s_qbf)
+    for i in range(4):
+        q, s = a_tile(i)
+        v.wait_ge(S["ld_a%d" % i], 16)
+        v.quantize_mx(q, s, T.a_sb[:, 512 * i:512 * i + 512]).then_inc(S["s_qa%d" % i], 1)
+
+    te.wait_ge(S.s_qbf, 1)
+    for i in range(4):
+        q, s = a_tile(i)
+        bqv, bsv = b_half(f0)
+        te.wait_ge(S["s_qa%d" % i], 1)
+        te.matmul_mx(bank(i), q, s, bqv, bsv, True, True).then_inc(S["s_pf%d" % i], 1)
+    for i in range(3):
+        sc.wait_ge(S["s_pf%d" % i], 1)
+        sc.activation(T.e[:, i:512:4], bank(i), copy).then_inc(S.s_cfs, 1)
+    v.wait_ge(S.s_pf3, 1)
+    v.tensor_copy(T.e[:, 3:512:4], bank(3)).then_inc(S.s_cfv, 1)
+    v.wait_ge(S.s_cfv, 1)
+    v.wait_ge(S.s_cfs, 3)
+    v.quantize_mx(T.tq[:, 0:HW], T.tsc[:, 0:HW], T.e[:, 0:512]).then_inc(S.s_tf, 1)
+
+    items = []
+    for d in far:
+        k = order[d].index(rank)
+        col = _land(T, topo, d, k)
+        if (rank, d) in relay:
+            items.append((relay[(rank, d)], S.rly_c, S.rly_s, PW * (d - f0), col))
+        else:
+            items.append((cores[d], S["arr%d" % k], S["arr%d" % k], PW * (d - f0), col))
+    g.wait_ge(S.s_tf, 1)
+    sent = _send(g, T, topo, core, items, T.tq, T.tsc)[1]
+
+    quant_b(n0, S.ld_bn, S.s_qbn)
+    te.wait_ge(S.s_qbn, 1)
+    for i in range(4):
+        q, s = a_tile(i)
+        bqv, bsv = b_half(n0)
+        te.matmul_mx(bank(4 + i), q, s, bqv, bsv, True, True).then_inc(S["s_pn%d" % i], 1)
+    for i in range(4):
+        if i % 2 == 0:
+            v.wait_ge(S["s_pn%d" % i], 1)
+            v.tensor_copy(T.e[:, 512 + i:1024:4], bank(4 + i)).then_inc(S.s_cnv, 1)
+        else:
+            sc.wait_ge(S["s_pn%d" % i], 1)
+            sc.activation(T.e[:, 512 + i:1024:4], bank(4 + i), copy).then_inc(S.s_cns, 1)
+    v.wait_ge(S.s_cnv, 2)
+    v.wait_ge(S.s_cns, 2)
+    v.quantize_mx(T.tq[:, HW:2 * HW], T.tsc[:, HW:2 * HW], T.e[:, 512:1024]).then_inc(S.s_tn, 1)
+    g.wait_ge(S.s_tn, 1)
+    for d in near:
+        if d != rank:
+            k = order[d].index(rank)
+            sent += _send(g, T, topo, core, [(cores[d], S["arr%d" % k], S["arr%d" % k], HW + PW * (d - n0),
+                                              _land(T, topo, d, k))], T.tq, T.tsc)[1]
+
+    te.wait_ge(S.s_cfv, 1)
+    te.wait_ge(S.s_cfs, 3)
+    for t in range(4):
+        q, s = a_tile(t)
+        bqv, bsv = b_half(n0)
+        te.matmul_mx(bank(t), q, s, bqv, bsv, True, False)
+    te.wait_ge(S.s_w, 1)
+    for k, s_rank in enumerate(order[rank]):
+        if (s_rank, rank) in relay:
+            inc = 2 * len(_engines(topo, relay[(s_rank, rank)], core))
+        else:
+            group = [x for x in range(N) if x != s_rank and topo.chip(cores[x]) == topo.chip(core)]
+            inc = 2 * _per(topo, cores[s_rank], [cores[x] for x in group])
+        te.wait_ge(S["arr%d" % k], inc)
+        first = _land(T, topo, rank, k) - PW * half
+        last = k == len(order[rank]) - 1
+        for t in range(4):
+            mm = te.matmul_mx(bank(t), T.wq[:, 128 * t:128 * t + 128], T.wsc[:, 128 * t:128 * t + 128],
+                              T.bq[:, first:first + HW], T.bsc[:, first:first + HW], False, last)
+            if last:
+                mm.then_inc(S["s_f%d" % t], 1)
+
+    for t in range(4):
+        src = T.ps[:, 512 * t + PW * half:512 * t + PW * half + PW]
+        if t % 2 == 0:
+            v.wait_ge(S["s_f%d" % t], 1)
+            v.tensor_copy(T.ysb[:, t:256:4], src).then_inc(S.s_yv, 1)
+        else:
+            sc.wait_ge(S["s_f%d" % t], 1)
+            sc.activation(T.ysb[:, t:256:4], src, copy).then_inc(S.s_ys, 1)
+    sy.wait_ge(S.s_yv, 2)
+    sy.wait_ge(S.s_ys, 2)
+    sy.dma_start(T.y[:], T.ysb[:]).then_inc(S.s_st, 16)
+    sy.wait_ge(S.s_st, 16)
+    g.wait_ge(S.sent, sent)

@@ -16,7 +16,7 @@ SCRATCH = {
     "bsc": ("sbuf", [128, B1 + 3 * PW], "uint8"),
     "ones": ("sbuf", [128, 128], "bfloat16"),
     "eye": ("sbuf", [128, 128], "bfloat16"),
-    "sel": ("sbuf", [128, 2048], "bfloat16"),
+    "sel": ("sbuf", [128, 516], "bfloat16"),
     "wq": ("sbuf", [128, 512], "float8_e4m3fn_x4"),
     "wsc": ("sbuf", [128, 512], "uint8"),
     "e": ("sbuf", [128, 1024], "bfloat16"),
@@ -25,9 +25,10 @@ SCRATCH = {
     "ysb": ("sbuf", [128, 256], "float32"),
     "ps": ("psum", [128, 4096], "float32"),
 }
+PIECES = [(0, 2), (2, 3), (3, 4)]
 SEMAPHORES = (
-    ["ld_bf", "ld_bn"] + ["ld_a%d" % i for i in range(4)]
-    + ["s_ones", "s_zero", "s_eye", "s_selc", "s_w", "s_qbf", "s_qbn"] + ["s_qa%d" % i for i in range(4)]
+    ["ld_bf", "ld_bn"] + ["ld_a%d" % i for i in range(3)]
+    + ["s_ones", "s_zero", "s_eye", "s_selc", "s_w", "s_qbf", "s_qbn"] + ["s_qa%d" % i for i in range(3)]
     + ["s_pf%d" % i for i in range(4)] + ["s_pn%d" % i for i in range(4)] + ["s_f%d" % i for i in range(4)]
     + ["s_cfv", "s_cfs", "s_tf", "s_cnv", "s_cns", "s_tn", "s_yv", "s_ys", "s_st"]
     + ["arr0", "arr1", "arr2", "rly_c", "rly_s", "sent"]
@@ -44,7 +45,7 @@ def _plan(T, topo):
                 continue
             cand = [h for h in range(topo.CHIPS * topo.CORES_PER_CHIP)
                     if h not in taken and topo.chip(h) == topo.chip(cores[s]) and topo.may_write(h, cores[d])]
-            cand.sort(key=lambda h: (topo.die(h) != topo.die(cores[s]), h))
+            cand.sort(key=lambda h: (topo.die(h) != topo.die(cores[d]), h))
             relay[(s, d)] = cand[0]
             taken.add(cand[0])
     order = {}
@@ -69,14 +70,38 @@ def _engines(topo, src, dst):
     return [x for x in range(m.bit_length()) if (m >> x) & 1]
 
 
-def _send(g, T, topo, core, items, src_q, src_s):
-    per = min(len(_engines(topo, core, it[0])) for it in items) // len(items)
+def _far_engines(T, topo, relay, s):
+    cores = list(T.cores)
+    dst = dict((d, relay.get((s, d), cores[d])) for d in range(N) if d not in _near(T, topo, s))
+    off = [d for d in dst if topo.chip(dst[d]) != topo.chip(cores[s])]
+    on = [d for d in dst if d not in off]
+    out = {}
+    used = []
+    for j, d in enumerate(off):
+        es = _engines(topo, cores[s], dst[d])
+        per = len(es) // len(off)
+        out[d] = es[j * per:(j + 1) * per]
+        used += out[d]
+    for j, d in enumerate(on):
+        es = [x for x in _engines(topo, cores[s], dst[d]) if x not in used]
+        per = len(es) // len(on)
+        out[d] = es[j * per:(j + 1) * per]
+    return out, used
+
+
+def _near_engines(T, topo, relay, s, d):
+    cores = list(T.cores)
+    used = _far_engines(T, topo, relay, s)[1]
+    return [x for x in _engines(topo, cores[s], cores[d]) if x not in used]
+
+
+def _send(g, T, topo, items, src_q, src_s):
     for what in range(2):
         trs = []
-        for j, (dc, sem_c, sem_s, a, b) in enumerate(items):
-            mask = sum(1 << x for x in _engines(topo, core, dc)[j * per:(j + 1) * per])
+        for (dc, sem_c, sem_s, a, b, es) in items:
+            mask = sum(1 << x for x in es)
             rid, pid, _se = topo.addr(dc)
-            if what == 0:
+            if what == 1:
                 src, dst, sem = src_q[:, a:a + PW].bitcast(dt.uint8), T.bq[:, b:b + PW].bitcast(dt.uint8), sem_c
             else:
                 src, dst, sem = src_s[:, a:a + PW], T.bsc[:, b:b + PW], sem_s
@@ -89,11 +114,7 @@ def _send(g, T, topo, core, items, src_q, src_s):
                 [RemoteDMATransfer(dst_ids=[DstId(rid=rid, pnc=pid)], dma_engine_mask=mask, remote_sem=sem,
                                    src=src, dst=dst) for (rid, pid, mask, sem, src, dst) in trs],
                 local_sem=T.sem.sent)
-    return per, 2 * per * len(items)
-
-
-def _per(topo, src, dsts):
-    return min(len(_engines(topo, src, d)) for d in dsts) // len(dsts)
+    return 2 * sum(len(it[5]) for it in items)
 
 
 def rank_program(g, core, T, topo):
@@ -106,17 +127,17 @@ def rank_program(g, core, T, topo):
         for (s, d), h in relay.items():
             if h != core:
                 continue
-            inc = _per(topo, cores[s], [relay[(s, x)] for x in range(N) if (s, x) in relay])
+            inc = len(_far_engines(T, topo, relay, s)[0][d])
             col = _land(T, topo, d, order[d].index(s))
             arr = S["arr%d" % order[d].index(s)]
             es = _engines(topo, core, cores[d])
             mask = sum(1 << x for x in es)
             rid, pid, _se = topo.addr(cores[d])
+            g.wait_ge(S.rly_s, inc)
+            g.remote_dma(T.bsc[:, col:col + PW], T.bsc[:, col:col + PW], arr, S.sent, pid, rid, mask)
             g.wait_ge(S.rly_c, inc)
             g.remote_dma(T.bq[:, col:col + PW].bitcast(dt.uint8), T.bq[:, col:col + PW].bitcast(dt.uint8),
                          arr, S.sent, pid, rid, mask)
-            g.wait_ge(S.rly_s, inc)
-            g.remote_dma(T.bsc[:, col:col + PW], T.bsc[:, col:col + PW], arr, S.sent, pid, rid, mask)
             g.wait_ge(S.sent, 2 * len(es))
         return
 
@@ -140,14 +161,14 @@ def rank_program(g, core, T, topo):
         q.dma_start(T.b_sb[:, 4 * PW * first:4 * PW * first + 4 * HW],
                     T.b[:, 4 * PW * first:4 * PW * first + 4 * HW]).then_inc(sem, 16)
 
-    def load_a(q, i):
-        q.dma_start(T.a_sb[:, 512 * i:512 * i + 512], T.a[:, 512 * i:512 * i + 512]).then_inc(S["ld_a%d" % i], 16)
+    def load_a(q, k):
+        lo, hi = PIECES[k]
+        q.dma_start(T.a_sb[:, 512 * lo:512 * hi], T.a[:, 512 * lo:512 * hi]).then_inc(S["ld_a%d" % k], 16)
 
     load_b(sy, f0, S.ld_bf)
     load_a(sc, 0)
     load_a(sy, 1)
     load_a(sc, 2)
-    load_a(sy, 3)
     load_b(sc, n0, S.ld_bn)
 
     v.memset(T.ones[:], 1.0).then_inc(S.s_ones, 1)
@@ -156,10 +177,7 @@ def rank_program(g, core, T, topo):
     g.affine_select(T.eye[:], T.ones[:], [[-1, 128]], AluOpType.is_equal, 0.0, 0, 1).then_inc(S.s_eye, 1)
     v.wait_ge(S.s_eye, 1)
     v.wait_ge(S.s_zero, 1)
-    for t in range(4):
-        v.tensor_copy(T.sel[:, 512 * t + t:512 * (t + 1):4], T.eye[:]).then_inc(S.s_selc, 1)
-    v.wait_ge(S.s_selc, 4)
-    v.quantize_mx(T.wq[:], T.wsc[:], T.sel[:]).then_inc(S.s_w, 1)
+    v.tensor_copy(T.sel[:, 3:512:4], T.eye[:]).then_inc(S.s_selc, 1)
 
     def quant_b(first, ld, sem):
         q, s = b_half(first)
@@ -167,17 +185,18 @@ def rank_program(g, core, T, topo):
         v.quantize_mx(q, s, T.b_sb[:, 4 * PW * first:4 * PW * first + 4 * HW]).then_inc(sem, 1)
 
     quant_b(f0, S.ld_bf, S.s_qbf)
-    for i in range(4):
-        q, s = a_tile(i)
-        v.wait_ge(S["ld_a%d" % i], 16)
-        v.quantize_mx(q, s, T.a_sb[:, 512 * i:512 * i + 512]).then_inc(S["s_qa%d" % i], 1)
+    for k, (lo, hi) in enumerate(PIECES):
+        v.wait_ge(S["ld_a%d" % k], 16)
+        v.quantize_mx(T.aq[:, 128 * lo:128 * hi], T.asc[:, 128 * lo:128 * hi],
+                      T.a_sb[:, 512 * lo:512 * hi]).then_inc(S["s_qa%d" % k], 1)
 
     te.wait_ge(S.s_qbf, 1)
-    for i in range(4):
-        q, s = a_tile(i)
-        bqv, bsv = b_half(f0)
-        te.wait_ge(S["s_qa%d" % i], 1)
-        te.matmul_mx(bank(i), q, s, bqv, bsv, True, True).then_inc(S["s_pf%d" % i], 1)
+    for k, (lo, hi) in enumerate(PIECES):
+        te.wait_ge(S["s_qa%d" % k], 1)
+        for i in range(lo, hi):
+            q, s = a_tile(i)
+            bqv, bsv = b_half(f0)
+            te.matmul_mx(bank(i), q, s, bqv, bsv, True, True).then_inc(S["s_pf%d" % i], 1)
     for i in range(3):
         sc.wait_ge(S["s_pf%d" % i], 1)
         sc.activation(T.e[:, i:512:4], bank(i), copy).then_inc(S.s_cfs, 1)
@@ -188,15 +207,16 @@ def rank_program(g, core, T, topo):
     v.quantize_mx(T.tq[:, 0:HW], T.tsc[:, 0:HW], T.e[:, 0:512]).then_inc(S.s_tf, 1)
 
     items = []
+    split = _far_engines(T, topo, relay, rank)[0]
     for d in far:
         k = order[d].index(rank)
         col = _land(T, topo, d, k)
         if (rank, d) in relay:
-            items.append((relay[(rank, d)], S.rly_c, S.rly_s, PW * (d - f0), col))
+            items.append((relay[(rank, d)], S.rly_c, S.rly_s, PW * (d - f0), col, split[d]))
         else:
-            items.append((cores[d], S["arr%d" % k], S["arr%d" % k], PW * (d - f0), col))
+            items.append((cores[d], S["arr%d" % k], S["arr%d" % k], PW * (d - f0), col, split[d]))
     g.wait_ge(S.s_tf, 1)
-    sent = _send(g, T, topo, core, items, T.tq, T.tsc)[1]
+    sent = _send(g, T, topo, items, T.tq, T.tsc)
 
     quant_b(n0, S.ld_bn, S.s_qbn)
     te.wait_ge(S.s_qbn, 1)
@@ -218,8 +238,13 @@ def rank_program(g, core, T, topo):
     for d in near:
         if d != rank:
             k = order[d].index(rank)
-            sent += _send(g, T, topo, core, [(cores[d], S["arr%d" % k], S["arr%d" % k], HW + PW * (d - n0),
-                                              _land(T, topo, d, k))], T.tq, T.tsc)[1]
+            sent += _send(g, T, topo, [(cores[d], S["arr%d" % k], S["arr%d" % k], HW + PW * (d - n0),
+                                        _land(T, topo, d, k), _near_engines(T, topo, relay, rank, d))], T.tq, T.tsc)
+
+    v.wait_ge(S.s_selc, 1)
+    for t in range(4):
+        v.quantize_mx(T.wq[:, 128 * t:128 * t + 128], T.wsc[:, 128 * t:128 * t + 128],
+                      T.sel[:, 3 - t:3 - t + 512]).then_inc(S.s_w, 1)
 
     te.wait_ge(S.s_cfv, 1)
     te.wait_ge(S.s_cfs, 3)
@@ -227,13 +252,14 @@ def rank_program(g, core, T, topo):
         q, s = a_tile(t)
         bqv, bsv = b_half(n0)
         te.matmul_mx(bank(t), q, s, bqv, bsv, True, False)
-    te.wait_ge(S.s_w, 1)
+    te.wait_ge(S.s_w, 4)
     for k, s_rank in enumerate(order[rank]):
         if (s_rank, rank) in relay:
             inc = 2 * len(_engines(topo, relay[(s_rank, rank)], core))
+        elif s_rank in near:
+            inc = 2 * len(_near_engines(T, topo, relay, s_rank, rank))
         else:
-            group = [x for x in range(N) if x != s_rank and topo.chip(cores[x]) == topo.chip(core)]
-            inc = 2 * _per(topo, cores[s_rank], [cores[x] for x in group])
+            inc = 2 * len(_far_engines(T, topo, relay, s_rank)[0][rank])
         te.wait_ge(S["arr%d" % k], inc)
         first = _land(T, topo, rank, k) - PW * half
         last = k == len(order[rank]) - 1

from concourse.bass import DstId, RemoteDMATransfer
from concourse.mybir import dt, AluOpType, ActivationFunctionType

N = 4
PW = 64
HW = 2 * PW
B0 = 3 * PW
B1 = B0 + N * PW

SCRATCH = {
    "a_sb": ("sbuf", [128, 2048], "bfloat16"),
    "b_sb": ("sbuf", [128, 1024], "bfloat16"),
    "aq": ("sbuf", [128, 512], "float8_e4m3fn_x4"),
    "asc": ("sbuf", [128, 512], "uint8"),
    "bq": ("sbuf", [128, B1 + 3 * PW], "float8_e4m3fn_x4"),
    "bsc": ("sbuf", [128, B1 + 3 * PW], "uint8"),
    "ones": ("sbuf", [128, 128], "bfloat16"),
    "eye": ("sbuf", [128, 128], "bfloat16"),
    "sel": ("sbuf", [128, 516], "bfloat16"),
    "wq": ("sbuf", [128, 512], "float8_e4m3fn_x4"),
    "wsc": ("sbuf", [128, 512], "uint8"),
    "e": ("sbuf", [128, 1024], "bfloat16"),
    "tq": ("sbuf", [128, 256], "float8_e4m3fn_x4"),
    "tsc": ("sbuf", [128, 256], "uint8"),
    "ysb": ("sbuf", [128, 256], "float32"),
    "ps": ("psum", [128, 4096], "float32"),
}
PIECES = [(0, 2), (2, 3), (3, 4)]
SEMAPHORES = (
    ["ld_bf", "ld_bn"] + ["ld_a%d" % i for i in range(3)]
    + ["s_ones", "s_zero", "s_eye", "s_selc", "s_w", "s_qbf", "s_qbn"] + ["s_qa%d" % i for i in range(3)]
    + ["s_pf%d" % i for i in range(4)] + ["s_pn%d" % i for i in range(4)] + ["s_f%d" % i for i in range(4)]
    + ["s_cfv", "s_cfs", "s_tf", "s_cnv", "s_cns", "s_tn", "s_yv", "s_ys", "s_st"]
    + ["arr0", "arr1", "arr2", "rly_c", "rly_s", "sent"]
)


def _plan(T, topo):
    cores = list(T.cores)
    taken = set(cores)
    relay = {}
    for s in range(N):
        for d in range(N):
            if s == d or topo.may_write(cores[s], cores[d]):
                continue
            cand = [h for h in range(topo.CHIPS * topo.CORES_PER_CHIP)
                    if h not in taken and topo.chip(h) == topo.chip(cores[s]) and topo.may_write(h, cores[d])]
            cand.sort(key=lambda h: (topo.die(h) != topo.die(cores[d]), h))
            relay[(s, d)] = cand[0]
            taken.add(cand[0])
    order = {}
    for d in range(N):
        snd = [s for s in range(N) if s != d]
        snd.sort(key=lambda s: (topo.chip(cores[s]) != topo.chip(cores[d]), (s, d) in relay, s))
        order[d] = snd
    return relay, order


def _near(T, topo, r):
    return [x for x in range(N) if topo.chip(T.cores[x]) == topo.chip(T.cores[r])]


def _land(T, topo, d, k):
    half = d - _near(T, topo, d)[0]
    return (B0 - PW - PW * k) if half == 0 else (B1 + PW * k)


def _engines(topo, src, dst):
    m = topo.mask(src, dst)
    return [x for x in range(m.bit_length()) if (m >> x) & 1]


def _far_engines(T, topo, relay, s):
    cores = list(T.cores)
    dst = dict((d, relay.get((s, d), cores[d])) for d in range(N) if d not in _near(T, topo, s))
    off = [d for d in dst if topo.chip(dst[d]) != topo.chip(cores[s])]
    on = [d for d in dst if d not in off]
    out = {}
    used = []
    for j, d in enumerate(off):
        es = _engines(topo, cores[s], dst[d])
        per = len(es) // len(off)
        out[d] = es[j * per:(j + 1) * per]
        used += out[d]
    for j, d in enumerate(on):
        es = [x for x in _engines(topo, cores[s], dst[d]) if x not in used]
        per = len(es) // len(on)
        out[d] = es[j * per:(j + 1) * per]
    return out, used


def _near_engines(T, topo, relay, s, d):
    cores = list(T.cores)
    used = _far_engines(T, topo, relay, s)[1]
    return [x for x in _engines(topo, cores[s], cores[d]) if x not in used]


def _send(g, T, topo, items, src_q, src_s):
    for what in range(2):
        trs = []
        for (dc, sem_c, sem_s, a, b, es) in items:
            mask = sum(1 << x for x in es)
            rid, pid, _se = topo.addr(dc)
            if what == 1:
                src, dst, sem = src_q[:, a:a + PW].bitcast(dt.uint8), T.bq[:, b:b + PW].bitcast(dt.uint8), sem_c
            else:
                src, dst, sem = src_s[:, a:a + PW], T.bsc[:, b:b + PW], sem_s
            trs.append((rid, pid, mask, sem, src, dst))
        if len(trs) == 1:
            rid, pid, mask, sem, src, dst = trs[0]
            g.remote_dma(dst, src, sem, T.sem.sent, pid, rid, mask)
        else:
            g.remote_dma_fused(
                [RemoteDMATransfer(dst_ids=[DstId(rid=rid, pnc=pid)], dma_engine_mask=mask, remote_sem=sem,
                                   src=src, dst=dst) for (rid, pid, mask, sem, src, dst) in trs],
                local_sem=T.sem.sent)
    return 2 * sum(len(it[5]) for it in items)


def rank_program(g, core, T, topo):
    relay, order = _plan(T, topo)
    cores = list(T.cores)
    S = T.sem
    rank = T.rank_of(core)

    if rank is None:
        for (s, d), h in relay.items():
            if h != core:
                continue
            inc = len(_far_engines(T, topo, relay, s)[0][d])
            col = _land(T, topo, d, order[d].index(s))
            arr = S["arr%d" % order[d].index(s)]
            es = _engines(topo, core, cores[d])
            mask = sum(1 << x for x in es)
            rid, pid, _se = topo.addr(cores[d])
            g.wait_ge(S.rly_s, inc)
            g.remote_dma(T.bsc[:, col:col + PW], T.bsc[:, col:col + PW], arr, S.sent, pid, rid, mask)
            g.wait_ge(S.rly_c, inc)
            g.remote_dma(T.bq[:, col:col + PW].bitcast(dt.uint8), T.bq[:, col:col + PW].bitcast(dt.uint8),
                         arr, S.sent, pid, rid, mask)
            g.wait_ge(S.sent, 2 * len(es))
        return

    v, sc, te, sy = g.vector, g.scalar, g.tensor, g.sync
    near = _near(T, topo, rank)
    far = [x for x in range(N) if x not in near]
    n0, f0 = near[0], far[0]
    half = rank - n0
    copy = ActivationFunctionType.Copy

    def bank(k):
        return T.ps[:, 512 * k:512 * k + HW]

    def a_tile(i):
        return T.aq[:, 128 * i:128 * i + 128], T.asc[:, 128 * i:128 * i + 128]

    def b_half(first):
        return T.bq[:, B0 + PW * first:B0 + PW * first + HW], T.bsc[:, B0 + PW * first:B0 + PW * first + HW]

    def load_b(q, first, sem):
        q.dma_start(T.b_sb[:, 4 * PW * first:4 * PW * first + 4 * HW],
                    T.b[:, 4 * PW * first:4 * PW * first + 4 * HW]).then_inc(sem, 16)

    def load_a(q, k):
        lo, hi = PIECES[k]
        q.dma_start(T.a_sb[:, 512 * lo:512 * hi], T.a[:, 512 * lo:512 * hi]).then_inc(S["ld_a%d" % k], 16)

    load_b(sy, f0, S.ld_bf)
    load_a(sc, 0)
    load_a(sy, 1)
    load_a(sc, 2)
    load_b(sc, n0, S.ld_bn)

    v.memset(T.ones[:], 1.0).then_inc(S.s_ones, 1)
    v.memset(T.sel[:], 0.0).then_inc(S.s_zero, 1)
    g.wait_ge(S.s_ones, 1)
    g.affine_select(T.eye[:], T.ones[:], [[-1, 128]], AluOpType.is_equal, 0.0, 0, 1).then_inc(S.s_eye, 1)
    v.wait_ge(S.s_eye, 1)
    v.wait_ge(S.s_zero, 1)
    v.tensor_copy(T.sel[:, 3:512:4], T.eye[:]).then_inc(S.s_selc, 1)

    def quant_b(first, ld, sem):
        q, s = b_half(first)
        v.wait_ge(ld, 16)
        v.quantize_mx(q, s, T.b_sb[:, 4 * PW * first:4 * PW * first + 4 * HW]).then_inc(sem, 1)

    quant_b(f0, S.ld_bf, S.s_qbf)
    for k, (lo, hi) in enumerate(PIECES):
        v.wait_ge(S["ld_a%d" % k], 16)
        v.quantize_mx(T.aq[:, 128 * lo:128 * hi], T.asc[:, 128 * lo:128 * hi],
                      T.a_sb[:, 512 * lo:512 * hi]).then_inc(S["s_qa%d" % k], 1)

    te.wait_ge(S.s_qbf, 1)
    for k, (lo, hi) in enumerate(PIECES):
        te.wait_ge(S["s_qa%d" % k], 1)
        for i in range(lo, hi):
            q, s = a_tile(i)
            bqv, bsv = b_half(f0)
            te.matmul_mx(bank(i), q, s, bqv, bsv, True, True).then_inc(S["s_pf%d" % i], 1)
    for i in range(3):
        sc.wait_ge(S["s_pf%d" % i], 1)
        sc.activation(T.e[:, i:512:4], bank(i), copy).then_inc(S.s_cfs, 1)
    v.wait_ge(S.s_pf3, 1)
    v.tensor_copy(T.e[:, 3:512:4], bank(3)).then_inc(S.s_cfv, 1)
    v.wait_ge(S.s_cfv, 1)
    v.wait_ge(S.s_cfs, 3)
    v.quantize_mx(T.tq[:, 0:HW], T.tsc[:, 0:HW], T.e[:, 0:512]).then_inc(S.s_tf, 1)

    items = []
    split = _far_engines(T, topo, relay, rank)[0]
    for d in far:
        k = order[d].index(rank)
        col = _land(T, topo, d, k)
        if (rank, d) in relay:
            items.append((relay[(rank, d)], S.rly_c, S.rly_s, PW * (d - f0), col, split[d]))
        else:
            items.append((cores[d], S["arr%d" % k], S["arr%d" % k], PW * (d - f0), col, split[d]))
    g.wait_ge(S.s_tf, 1)
    sent = _send(g, T, topo, items, T.tq, T.tsc)

    quant_b(n0, S.ld_bn, S.s_qbn)
    te.wait_ge(S.s_qbn, 1)
    for i in range(4):
        q, s = a_tile(i)
        bqv, bsv = b_half(n0)
        te.matmul_mx(bank(4 + i), q, s, bqv, bsv, True, True).then_inc(S["s_pn%d" % i], 1)
    for i in range(4):
        if i % 2 == 0:
            v.wait_ge(S["s_pn%d" % i], 1)
            v.tensor_copy(T.e[:, 512 + i:1024:4], bank(4 + i)).then_inc(S.s_cnv, 1)
        else:
            sc.wait_ge(S["s_pn%d" % i], 1)
            sc.activation(T.e[:, 512 + i:1024:4], bank(4 + i), copy).then_inc(S.s_cns, 1)
    v.wait_ge(S.s_cnv, 2)
    v.wait_ge(S.s_cns, 2)
    v.quantize_mx(T.tq[:, HW:2 * HW], T.tsc[:, HW:2 * HW], T.e[:, 512:1024]).then_inc(S.s_tn, 1)
    g.wait_ge(S.s_tn, 1)
    for d in near:
        if d != rank:
            k = order[d].index(rank)
            sent += _send(g, T, topo, [(cores[d], S["arr%d" % k], S["arr%d" % k], HW + PW * (d - n0),
                                        _land(T, topo, d, k), _near_engines(T, topo, relay, rank, d))], T.tq, T.tsc)

    v.wait_ge(S.s_selc, 1)
    for t in range(4):
        v.quantize_mx(T.wq[:, 128 * t:128 * t + 128], T.wsc[:, 128 * t:128 * t + 128],
                      T.sel[:, 3 - t:3 - t + 512]).then_inc(S.s_w, 1)

    te.wait_ge(S.s_cfv, 1)
    te.wait_ge(S.s_cfs, 3)
    for t in range(4):
        q, s = a_tile(t)
        bqv, bsv = b_half(n0)
        te.matmul_mx(bank(t), q, s, bqv, bsv, True, False)
    te.wait_ge(S.s_w, 4)
    for k, s_rank in enumerate(order[rank]):
        if (s_rank, rank) in relay:
            inc = 2 * len(_engines(topo, relay[(s_rank, rank)], core))
        elif s_rank in near:
            inc = 2 * len(_near_engines(T, topo, relay, s_rank, rank))
        else:
            inc = 2 * len(_far_engines(T, topo, relay, s_rank)[0][rank])
        te.wait_ge(S["arr%d" % k], inc)
        first = _land(T, topo, rank, k) - PW * half
        last = k == len(order[rank]) - 1
        for t in range(4):
            mm = te.matmul_mx(bank(t), T.wq[:, 128 * t:128 * t + 128], T.wsc[:, 128 * t:128 * t + 128],
                              T.bq[:, first:first + HW], T.bsc[:, first:first + HW], False, last)
            if last:
                mm.then_inc(S["s_f%d" % t], 1)

    for t in range(4):
        src = T.ps[:, 512 * t + PW * half:512 * t + PW * half + PW]
        if t % 2 == 0:
            v.wait_ge(S["s_f%d" % t], 1)
            v.tensor_copy(T.ysb[:, t:256:4], src).then_inc(S.s_yv, 1)
        else:
            sc.wait_ge(S["s_f%d" % t], 1)
            sc.activation(T.ysb[:, t:256:4], src, copy).then_inc(S.s_ys, 1)
    sy.wait_ge(S.s_yv, 2)
    sy.wait_ge(S.s_ys, 2)
    sy.dma_start(T.y[:], T.ysb[:]).then_inc(S.s_st, 16)
    sy.wait_ge(S.s_st, 16)
    g.wait_ge(S.sent, sent)
